import numpy as np
import ml_dtypes


def mxq(x, axis, fmt="e4m3"):
    dtype, down = {"e4m3": (ml_dtypes.float8_e4m3fn, 7), "e5m2": (ml_dtypes.float8_e5m2, 14)}[fmt]
    v = np.moveaxis(np.asarray(x, np.float32).astype(ml_dtypes.bfloat16).astype(np.float64), axis, -1)
    blocks = v.reshape(v.shape[:-1] + (-1, 32))
    amax = np.abs(blocks).max(-1, keepdims=True)
    byte = np.maximum(np.where(amax > 0, np.frexp(amax)[1] - 1 + 127, 0) - down, 1)
    scale = np.exp2(byte - 127.0)
    codes = (blocks / scale).astype(np.float32).astype(dtype).astype(np.float64)
    return np.moveaxis((codes * scale).reshape(v.shape), -1, axis)


WIDE = False


def mx_kscale(k):
    if not WIDE:
        return np.ones(k)
    levels = np.array([10, -10, 5, -5, 0])
    if k % 512:
        return np.exp2(np.random.permutation(np.resize(levels, k // 32))).repeat(32)
    a = np.empty((k // 512, 16))
    for p in range(k // 512):
        a[p, :8] = np.random.permutation(np.resize(levels, 8))
        for g in range(8):
            far = levels[np.abs(levels - a[p, g]) >= 10]
            a[p, g + 8] = far[np.random.randint(len(far))]
    return np.exp2(a.ravel()).repeat(32)


def f64(x):
    return np.asarray(x).astype(np.float64)


def striped(idx):
    return np.tile(idx.reshape(-1, 16).T, (8, 1)).astype(np.uint16)


def unstriped(offs):
    return offs[:16].T.reshape(-1).astype(np.int64)


def pack_weight(w):
    k, n = w.shape
    w = f64(np.asarray(w, np.float32).astype(ml_dtypes.bfloat16)).reshape(k // 32, 32, n)
    amax = np.abs(w).max(1)
    byte = np.clip(np.where(amax > 0, np.frexp(amax)[1] - 1 + 127 - 7, 1), 1, 254)
    scaled = (w * np.exp2(127.0 - byte)[:, None, :]).reshape(k, n).astype(np.float32)
    words = np.ascontiguousarray(scaled.reshape(k // 512, 128, 4, n).transpose(0, 1, 3, 2)).astype(ml_dtypes.float8_e4m3fn).view(np.uint8)
    return words, np.ascontiguousarray(byte.astype(np.uint8).reshape(k // 512, 16, n))


def unpack_weight(words, scales):
    g, p, n, _ = words.shape
    vals = np.ascontiguousarray(words).view(ml_dtypes.float8_e4m3fn).astype(np.float64) * np.repeat(np.exp2(scales.astype(np.float64) - 127.0), 8, axis=1)[..., None]
    return vals.transpose(0, 1, 3, 2).reshape(g * 512, n)


E2M1 = np.array([0.0, 0.5, 1.0, 1.5, 2.0, 3.0, 4.0, 6.0, -0.0, -0.5, -1.0, -1.5, -2.0, -3.0, -4.0, -6.0])


def pack_fp4(w):
    k, n = w.shape
    w = f64(np.asarray(w, np.float32).astype(ml_dtypes.bfloat16)).reshape(k // 32, 32, n)
    amax = np.abs(w).max(1)
    mant, ex = np.frexp(amax / 6.0)
    byte = np.clip(np.where(amax > 0, np.where(mant > 0.5, ex, ex - 1) + 127, 1), 1, 254)
    scaled = (w * np.exp2(127.0 - byte)[:, None, :]).reshape(k, n).astype(np.float32)
    c = np.ascontiguousarray(scaled.reshape(k // 512, 128, 4, n).transpose(0, 1, 3, 2)).astype(ml_dtypes.float4_e2m1fn).view(np.uint8) & 0xF
    words = (c[..., 0::2] | (c[..., 1::2] << 4)).reshape(k // 512, 128, 2 * n)
    return np.ascontiguousarray(words), np.ascontiguousarray(byte.astype(np.uint8).reshape(k // 512, 16, n))


def unpack_fp4(words, scales):
    g, _, n = scales.shape
    words = np.ascontiguousarray(words).reshape(g, 128, n, 2)
    nib = np.empty((g, 128, n, 4), np.uint8)
    nib[..., 0::2] = words & 0xF
    nib[..., 1::2] = words >> 4
    vals = E2M1[nib] * np.repeat(np.exp2(scales.astype(np.float64) - 127.0), 8, axis=1)[..., None]
    return vals.transpose(0, 1, 3, 2).reshape(g * 512, n)


def relu(v):
    return np.maximum(v, 0.0)


K, T, S, D, N, H, V, U = 1024, 4096, 1024, 4, 256, 512, 256, 512


def setup_inputs():
    n = np.random.standard_normal
    s = mx_kscale(K)[:, None]
    u = mx_kscale(H)
    packed_xT = pack_weight(n((K, T)) * s)
    packed_w1 = pack_fp4(n((K, H)) / np.sqrt(K) / s)
    packed_w2 = pack_fp4(n((H, N)) / np.sqrt(H) / u[:, None])
    return {
        "x_words": packed_xT[0],
        "x_scales": packed_xT[1],
        "w1_words": packed_w1[0],
        "w1_scales": packed_w1[1],
        "dist": (np.random.uniform(0.1, 1.2, (H, S))).astype(np.float32),
        "brdf": (np.random.uniform(0.2, 1.2, (H, U))).astype(np.float32),
        "unit": (np.random.uniform(0.6, 1.4, (H, 1)) * u[:, None]).astype(np.float32),
        "w2_words": packed_w2[0],
        "w2_scales": packed_w2[1],
        "offs": striped(np.random.permutation(T)[:S]),
        "pix": striped(np.random.permutation(np.concatenate([np.arange(V), np.random.randint(0, V, U - V)]))),
    }


def reference(x_words, x_scales, w1_words, w1_scales, dist, brdf, unit, w2_words, w2_scales, offs, pix):
    xq = unpack_weight(x_words, x_scales)[:, unstriped(offs)]
    y = unpack_fp4(w1_words, w1_scales).T @ xq
    flux = np.log(np.exp(y) + 1.0)
    cone = relu(-1.0 * f64(dist) + 1.0)
    fw = flux * cone
    num = fw.reshape(len(fw), -1, D).sum(axis=2)
    rad = f64(dist).reshape(len(f64(dist)), -1, D).max(axis=2)
    est = num / ((rad) ** 2 + 0.2)
    ep = est[:, unstriped(pix)]
    rad2 = ep * f64(brdf)
    hid = f64(unit) * np.log(rad2 + 0.3)
    return unpack_fp4(w2_words, w2_scales).T @ mxq(hid, 0, "e4m3")

@@ -1,0 +1,213 @@
+from contextlib import ExitStack
+
+import concourse.mybir as mybir
+
+K, T, S, D, N, H, V, U = 1024, 4096, 1024, 4, 256, 512, 256, 512
+FLOPS = 2 * K * H * S + 2 * H * N * U
+
+F32 = mybir.dt.float32
+BF16 = mybir.dt.bfloat16
+I32 = mybir.dt.int32
+U32 = mybir.dt.uint32
+U16 = mybir.dt.uint16
+U8 = mybir.dt.uint8
+FP8X4 = mybir.dt.float8_e4m3fn_x4
+FP4X4 = mybir.dt.float4_e2m1fn_x4
+ALU = mybir.AluOpType
+ACT = mybir.ActivationFunctionType
+
+P = 128
+PACK = 4
+PASSES = K // (P * PACK)
+BANK = 512
+HALVES = S // BANK
+QUADS = 4
+ROWS = 4
+TINY = 2.0 ** -60
+PIX_HALF = U // 2
+
+
+def tile_picked_yphotn_log_p_kernel(
+    tc, x_words, x_scales, w1_words, w1_scales, dist, brdf, unit, w2_words, w2_scales, offs, pix, out
+):
+    nc = tc.nc
+    dist_rows = dist.rearrange("(p t) j -> p t j", t=PACK)
+
+    with ExitStack() as ctx:
+        keep = ctx.enter_context(tc.tile_pool(name="keep", bufs=1))
+        psum = ctx.enter_context(tc.psum_pool(name="psum", bufs=1))
+
+        offs_sb = keep.tile([P, S // 16], U16, name="offs_sb")
+        nc.sync.dma_start(offs_sb[:], offs)
+        w1_raw = keep.tile([P, PASSES, 2 * H], U8, name="w1_raw", tag="slot_a", align_bytes=64)
+        nc.sync.dma_start(out=w1_raw[:].bitcast(I32), in_=w1_words.rearrange("o p b -> p o b").bitcast(I32))
+        pix_sb = keep.tile([P, U // 16], U16, name="pix_sb")
+        nc.sync.dma_start(pix_sb[:], pix)
+        x_first = keep.tile([P, T], U32, name="x_first", tag="slot_c", align_bytes=64)
+        nc.sync.dma_start(out=x_first[:].bitcast(I32), in_=x_words[0].rearrange("p n t -> p (n t)").bitcast(I32))
+
+        xs_win = keep.tile([P, T], U8, name="xs_win", tag="slot_b", align_bytes=64)
+        nc.vector.memset(xs_win[:].bitcast(I32), 0)
+        for q in range(QUADS):
+            nc.scalar.dma_start(
+                out=xs_win[32 * q : 32 * q + PASSES * ROWS, :].bitcast(I32),
+                in_=x_scales[:, ROWS * q : ROWS * (q + 1), :].bitcast(I32),
+            )
+        w1s_raw = keep.tile([P, PASSES, H], U8, name="w1s_raw", align_bytes=64)
+        nc.gpsimd.memset(w1s_raw[:].bitcast(I32), 0)
+        for q in range(QUADS):
+            (nc.gpsimd if q < 2 else nc.scalar).dma_start(
+                out=w1s_raw[32 * q : 32 * q + ROWS].bitcast(I32),
+                in_=w1_scales[:, ROWS * q : ROWS * (q + 1), :].rearrange("o r n -> r o n").bitcast(I32),
+            )
+        xs_second = keep.tile([P, S], U8, name="xs_second", align_bytes=64)
+        nc.gpsimd.memset(xs_second[:].bitcast(I32), 0)
+        w2s = keep.tile([P, N], U8, name="w2s", align_bytes=64)
+        nc.gpsimd.memset(w2s[:].bitcast(I32), 0)
+
+        w1d = keep.tile([P, PASSES, PACK, P, 2], U8, name="w1d", align_bytes=64)
+        nc.vector.tensor_copy(out=w1d[:], in_=w1_raw[:].rearrange("p o (m t b) -> p o t m b", t=PACK, b=2))
+        x_second = keep.tile([P, T], U32, name="x_second", tag="slot_a", align_bytes=64)
+        nc.sync.dma_start(out=x_second[:].bitcast(I32), in_=x_words[1].rearrange("p n t -> p (n t)").bitcast(I32))
+        x_win = [x_first, x_second]
+        xs_both = keep.tile([P, S], U8, name="xs_both", align_bytes=64)
+        nc.vector.tensor_copy(out=xs_both[:], in_=xs_win[:].indirect(offs_sb[:]))
+        for q in range(QUADS):
+            nc.scalar.dma_start(
+                out=xs_second[32 * q : 32 * q + ROWS, :].bitcast(I32),
+                in_=xs_both[32 * q + ROWS : 32 * q + 2 * ROWS, :].bitcast(I32),
+            )
+        xs = [xs_both, xs_second]
+        w1sd = keep.tile([P, PASSES, PACK, P], U8, name="w1sd", align_bytes=64)
+        nc.vector.tensor_copy(out=w1sd[:], in_=w1s_raw[:].rearrange("p o (m t) -> p o t m", t=PACK))
+
+        dist_a = keep.tile([P, S], F32, name="dist_a", tag="slot_b", align_bytes=64)
+        nc.sync.dma_start(out=dist_a[:], in_=dist_rows[:, 0, :])
+
+        y = {}
+        for h in range(HALVES):
+            for t in range(PACK):
+                y[t, h] = psum.tile([P, BANK], F32, name="y%d%d" % (t, h), tag="bank%d" % (PACK * h + t))
+        for o in range(PASSES):
+            for h in range(HALVES):
+                cols = slice(h * BANK, (h + 1) * BANK)
+                xg = keep.tile([P, BANK], U32, name="xg%d%d" % (o, h), align_bytes=64)
+                nc.vector.tensor_copy(
+                    out=xg[:], in_=x_win[o][:].indirect(offs_sb[:, h * BANK // 16 : (h + 1) * BANK // 16])
+                )
+                for t in range(PACK):
+                    nc.tensor.matmul_mx(
+                        out=y[t, h][:],
+                        lhsT=w1d[:, o, t].rearrange("p m b -> p (m b)").bitcast(FP4X4),
+                        lhsT_scale=w1sd[:, o, t, :],
+                        rhs=xg[:].bitcast(FP8X4),
+                        rhs_scale=xs[o][:, cols],
+                        start=(o == 0),
+                        stop=(o == PASSES - 1),
+                    )
+
+        late = keep.tile([P, 3 * S + PACK * U], F32, name="late", tag="slot_c", align_bytes=64)
+        for t in range(1, PACK):
+            nc.sync.dma_start(out=late[:, (t - 1) * S : t * S], in_=dist_rows[:, t, :])
+        nc.sync.dma_start(out=late[:, 3 * S :], in_=brdf.rearrange("(p t) r -> p (t r)", t=PACK))
+        dist_sb = [dist_a[:]] + [late[:, (t - 1) * S : t * S] for t in range(1, PACK)]
+
+        unit_sb = keep.tile([P, PACK], F32, name="unit_sb")
+        nc.gpsimd.dma_start(out=unit_sb[:], in_=unit.rearrange("(p t) o -> p (t o)", t=PACK))
+        w2 = keep.tile([P, 2 * N], U8, name="w2", align_bytes=64)
+        nc.gpsimd.dma_start(out=w2[:].bitcast(I32), in_=w2_words[0].bitcast(I32))
+        for q in range(QUADS):
+            nc.gpsimd.dma_start(
+                out=w2s[32 * q : 32 * q + ROWS, :].bitcast(I32),
+                in_=w2_scales[0, ROWS * q : ROWS * (q + 1), :].bitcast(I32),
+            )
+
+        sig = [keep.tile([P, D, HALVES, BANK // D], F32, name="sig%d" % t) for t in range(PACK)]
+        for h in range(HALVES):
+            for t in range(PACK):
+                nc.scalar.activation(
+                    out=sig[t][:, :, h, :], in_=y[t, h][:].rearrange("p (v d) -> p d v", d=D), func=ACT.Sigmoid, scale=-1.0
+                )
+
+        rad = keep.tile([P, PACK, V], F32, name="rad")
+        slope = [keep.tile([P, S], F32, name="slope%d" % t) for t in range(PACK)]
+        for t in range(PACK):
+            nc.vector.tensor_reduce(
+                out=rad[:, t, :], in_=dist_sb[t].rearrange("p (v d) -> p v d", d=D), axis=mybir.AxisListType.X, op=ALU.max
+            )
+            nc.gpsimd.tensor_scalar(
+                out=slope[t][:].rearrange("p (d c i) -> p c d i", d=D, i=4),
+                in0=dist_sb[t].rearrange("p (c i d) -> p c d i", d=D, i=4),
+                scalar1=-1.0, scalar2=1.0, op0=ALU.mult, op1=ALU.add,
+            )
+        rad_sq = keep.tile([P, PACK, V], F32, name="rad_sq")
+        nc.vector.tensor_tensor(out=rad_sq[:], in0=rad[:], in1=rad[:], op=ALU.mult)
+
+        logsig = [keep.tile([P, D, HALVES, BANK // D], F32, name="logsig%d" % t) for t in range(PACK)]
+        for t in range(PACK):
+            nc.scalar.activation(out=logsig[t][:], in_=sig[t][:], func=ACT.Ln, bias=TINY)
+        log_sq = keep.tile([P, PACK, V], F32, name="log_sq")
+        nc.scalar.activation(out=log_sq[:], in_=rad_sq[:], func=ACT.Ln, scale=5.0, bias=TINY)
+        inv = keep.tile([P, PACK, V], F32, name="inv")
+        nc.scalar.activation(out=inv[:], in_=log_sq[:], func=ACT.Sigmoid, scale=-1.0)
+
+        hid = keep.tile([P, PACK, U], BF16, name="hid", align_bytes=64)
+        for t in range(PACK):
+            nflux = keep.tile([P, D, HALVES, BANK // D], F32, name="nflux%d" % t)
+            for h in range(HALVES):
+                nc.vector.scalar_tensor_tensor(
+                    out=nflux[:, :, h, :], in0=y[t, h][:].rearrange("p (v d) -> p d v", d=D), scalar=-1.0,
+                    in1=logsig[t][:, :, h, :], op0=ALU.mult, op1=ALU.min,
+                )
+            fw = keep.tile([P, S], F32, name="fw%d" % t)
+            nc.vector.scalar_tensor_tensor(
+                out=fw[:], in0=slope[t][:], scalar=0.0, in1=nflux[:].rearrange("p d h v -> p (d h v)"),
+                op0=ALU.max, op1=ALU.mult,
+            )
+            est = keep.tile([P, 3 * V], F32, name="est%d" % t)
+            nc.vector.tensor_tensor(out=est[:, V:], in0=fw[:, : 2 * V], in1=fw[:, 2 * V :], op=ALU.add)
+            num = keep.tile([P, V], F32, name="num%d" % t)
+            nc.vector.tensor_tensor(out=num[:], in0=est[:, V : 2 * V], in1=est[:, 2 * V :], op=ALU.add)
+            nc.vector.tensor_tensor(out=est[:, :V], in0=num[:], in1=inv[:, t, :], op=ALU.mult)
+            ep = keep.tile([P, U], F32, name="ep%d" % t)
+            nc.scalar.activation(out=ep[:], in_=est[:].indirect(pix_sb[:]), func=ACT.Copy)
+            rad2 = keep.tile([P, U], F32, name="rad2%d" % t)
+            nc.vector.tensor_tensor(
+                out=rad2[:], in0=ep[:], in1=late[:, 3 * S + t * U : 3 * S + (t + 1) * U], op=ALU.mult
+            )
+            logr = keep.tile([P, U], F32, name="logr%d" % t)
+            nc.scalar.activation(out=logr[:], in_=rad2[:], func=ACT.Ln, scale=-5.0, bias=0.3)
+            nc.vector.tensor_scalar(
+                out=hid[:, t, :], in0=logr[:], scalar1=unit_sb[:, t : t + 1], scalar2=None, op0=ALU.mult
+            )
+
+        out_rows = out.rearrange("(b p) r -> p b r", p=P)
+        for g in range(U // PIX_HALF):
+            cols = slice(g * PIX_HALF, (g + 1) * PIX_HALF)
+            woven = keep.tile([P, PIX_HALF, PACK], BF16, name="woven%d" % g, align_bytes=64)
+            nc.vector.tensor_copy(
+                out=woven[:].rearrange("p (c i) t -> p c t i", i=4),
+                in_=hid[:, :, cols].rearrange("p t (c i) -> p c t i", i=4),
+            )
+            codes = keep.tile([P, PIX_HALF], U32, name="codes%d" % g, align_bytes=64)
+            scales = keep.tile([P, PIX_HALF], U8, name="scales%d" % g, align_bytes=64)
+            nc.vector.quantize_mx(
+                out=codes[:].bitcast(FP8X4), scales=scales[:], in_=woven[:].rearrange("p r t -> p (r t)")
+            )
+            res = keep.tile([P, N // P, PIX_HALF], F32, name="res%d" % g)
+            for b in range(N // P):
+                acc = psum.tile([P, PIX_HALF], F32, name="acc%d%d" % (g, b), tag="bank%d" % (2 * g + b))
+                nc.tensor.matmul_mx(
+                    out=acc[:],
+                    lhsT=w2[:, 2 * P * b : 2 * P * (b + 1)].bitcast(FP4X4),
+                    lhsT_scale=w2s[:, P * b : P * (b + 1)],
+                    rhs=codes[:].bitcast(FP8X4),
+                    rhs_scale=scales[:],
+                    start=True,
+                    stop=True,
+                )
+                if b == 0:
+                    nc.scalar.copy(out=res[:, b, :], in_=acc[:])
+                else:
+                    nc.vector.tensor_copy(out=res[:, b, :], in_=acc[:])
+            nc.sync.dma_start(out=out_rows[:, :, cols], in_=res[:])

@@ -1,6 +1,8 @@
+import math
 from contextlib import ExitStack
 
 import concourse.mybir as mybir
+from concourse.masks import make_identity
 
 K, T, S, D, N, H, V, U = 1024, 4096, 1024, 4, 256, 512, 256, 512
 FLOPS = 2 * K * H * S + 2 * H * N * U
@@ -25,6 +27,8 @@ QUADS = 4
 ROWS = 4
 TINY = 2.0 ** -60
 PIX_HALF = U // 2
+KNEE = 16.0
+SIG_FLOOR = 1.0 / (1.0 + math.exp(KNEE))
 
 
 def tile_picked_yphotn_log_p_kernel(
@@ -37,52 +41,97 @@ def tile_picked_yphotn_log_p_kernel(
         keep = ctx.enter_context(tc.tile_pool(name="keep", bufs=1))
         psum = ctx.enter_context(tc.psum_pool(name="psum", bufs=1))
 
+        ident = keep.tile([P, P], F32, name="ident")
+        make_identity(nc, ident[:])
+
         offs_sb = keep.tile([P, S // 16], U16, name="offs_sb")
         nc.sync.dma_start(offs_sb[:], offs)
         w1_raw = keep.tile([P, PASSES, 2 * H], U8, name="w1_raw", tag="slot_a", align_bytes=64)
         nc.sync.dma_start(out=w1_raw[:].bitcast(I32), in_=w1_words.rearrange("o p b -> p o b").bitcast(I32))
         pix_sb = keep.tile([P, U // 16], U16, name="pix_sb")
         nc.sync.dma_start(pix_sb[:], pix)
-        x_first = keep.tile([P, T], U32, name="x_first", tag="slot_c", align_bytes=64)
-        nc.sync.dma_start(out=x_first[:].bitcast(I32), in_=x_words[0].rearrange("p n t -> p (n t)").bitcast(I32))
+        dist_sb = [keep.tile([P, S], F32, name="dist%d" % t, tag="dist%d" % t) for t in range(PACK)]
+        nc.sync.dma_start(out=dist_sb[0][:], in_=dist_rows[:, 0, :])
 
         xs_win = keep.tile([P, T], U8, name="xs_win", tag="slot_b", align_bytes=64)
         nc.vector.memset(xs_win[:].bitcast(I32), 0)
+        nc.sync.dma_start(out=xs_win[0:P:4, :].bitcast(I32), in_=x_scales.rearrange("o s n -> s o n").bitcast(I32))
+        for t in range(1, PACK):
+            nc.sync.dma_start(out=dist_sb[t][:], in_=dist_rows[:, t, :])
+        w1s_raw = keep.tile([P, PASSES * H], U8, name="w1s_raw", tag="slot_c", align_bytes=64)
+        nc.vector.memset(w1s_raw[:].bitcast(I32), 0)
         for q in range(QUADS):
-            nc.scalar.dma_start(
-                out=xs_win[32 * q : 32 * q + PASSES * ROWS, :].bitcast(I32),
-                in_=x_scales[:, ROWS * q : ROWS * (q + 1), :].bitcast(I32),
-            )
-        w1s_raw = keep.tile([P, PASSES, H], U8, name="w1s_raw", align_bytes=64)
-        nc.gpsimd.memset(w1s_raw[:].bitcast(I32), 0)
-        for q in range(QUADS):
-            (nc.gpsimd if q < 2 else nc.scalar).dma_start(
-                out=w1s_raw[32 * q : 32 * q + ROWS].bitcast(I32),
+            nc.sync.dma_start(
+                out=w1s_raw[32 * q : 32 * q + ROWS, :].bitcast(I32),
                 in_=w1_scales[:, ROWS * q : ROWS * (q + 1), :].rearrange("o r n -> r o n").bitcast(I32),
             )
-        xs_second = keep.tile([P, S], U8, name="xs_second", align_bytes=64)
-        nc.gpsimd.memset(xs_second[:].bitcast(I32), 0)
-        w2s = keep.tile([P, N], U8, name="w2s", align_bytes=64)
-        nc.gpsimd.memset(w2s[:].bitcast(I32), 0)
+        xs = keep.tile([P, PASSES * S], U8, name="xs", align_bytes=64)
+        nc.vector.memset(xs[:].bitcast(I32), 0)
 
         w1d = keep.tile([P, PASSES, PACK, P, 2], U8, name="w1d", align_bytes=64)
         nc.vector.tensor_copy(out=w1d[:], in_=w1_raw[:].rearrange("p o (m t b) -> p o t m b", t=PACK, b=2))
-        x_second = keep.tile([P, T], U32, name="x_second", tag="slot_a", align_bytes=64)
+        x_first = keep.tile([P, T], U32, name="x_first", tag="slot_a", align_bytes=64)
+        nc.sync.dma_start(out=x_first[:].bitcast(I32), in_=x_words[0].rearrange("p n t -> p (n t)").bitcast(I32))
+        xs_spread = keep.tile([P, S], U8, name="xs_spread", tag="slot_d", align_bytes=64)
+        nc.vector.tensor_copy(out=xs_spread[:], in_=xs_win[:].indirect(offs_sb[:]))
+        for q in range(QUADS):
+            nc.sync.dma_start(
+                out=xs[32 * q : 32 * q + ROWS, :].bitcast(I32),
+                in_=xs_spread[32 * q : 32 * (q + 1) : 4, :].bitcast(I32),
+            )
+        x_second = keep.tile([P, T], U32, name="x_second", tag="slot_b", align_bytes=64)
         nc.sync.dma_start(out=x_second[:].bitcast(I32), in_=x_words[1].rearrange("p n t -> p (n t)").bitcast(I32))
         x_win = [x_first, x_second]
-        xs_both = keep.tile([P, S], U8, name="xs_both", align_bytes=64)
-        nc.vector.tensor_copy(out=xs_both[:], in_=xs_win[:].indirect(offs_sb[:]))
-        for q in range(QUADS):
-            nc.scalar.dma_start(
-                out=xs_second[32 * q : 32 * q + ROWS, :].bitcast(I32),
-                in_=xs_both[32 * q + ROWS : 32 * q + 2 * ROWS, :].bitcast(I32),
-            )
-        xs = [xs_both, xs_second]
         w1sd = keep.tile([P, PASSES, PACK, P], U8, name="w1sd", align_bytes=64)
-        nc.vector.tensor_copy(out=w1sd[:], in_=w1s_raw[:].rearrange("p o (m t) -> p o t m", t=PACK))
+        nc.vector.tensor_copy(out=w1sd[:], in_=w1s_raw[:].rearrange("p (o m t) -> p o t m", o=PASSES, t=PACK))
 
-        dist_a = keep.tile([P, S], F32, name="dist_a", tag="slot_b", align_bytes=64)
-        nc.sync.dma_start(out=dist_a[:], in_=dist_rows[:, 0, :])
+        rad = keep.tile([P, PACK, V], F32, name="rad")
+        cone = [keep.tile([P, S], F32, name="cone%d" % t) for t in range(PACK)]
+        for t in range(PACK):
+            nc.vector.tensor_reduce(
+                out=rad[:, t, :], in_=dist_sb[t][:].rearrange("p (v d) -> p v d", d=D), axis=mybir.AxisListType.X, op=ALU.max
+            )
+            nc.scalar.activation(
+                out=cone[t][:].rearrange("p (d c i) -> p c d i", d=D, i=4),
+                in_=dist_sb[t][:].rearrange("p (c i d) -> p c d i", d=D, i=4),
+                func=ACT.Relu, scale=-1.0, bias=1.0,
+            )
+        rad_sq = keep.tile([P, PACK, V], F32, name="rad_sq", tag="slot_e")
+        log_sq = keep.tile([P, PACK, V], F32, name="log_sq")
+        for t in range(PACK):
+            nc.scalar.activation(out=rad_sq[:, t, :], in_=rad[:, t, :], func=ACT.Square)
+            nc.scalar.activation(out=log_sq[:, t, :], in_=rad_sq[:, t, :], func=ACT.Ln, scale=5.0, bias=TINY)
+        cone4 = [c[:].rearrange("p (d h v) -> p d h v", d=D, h=HALVES) for c in cone]
+        knee_t = keep.tile([P, HALVES, PACK, P], F32, name="knee_t")
+        for h in range(HALVES):
+            bank = psum.tile([P, PACK, P], F32, name="cone_sum%d" % h, tag="bank%d" % h)
+            for t in range(PACK):
+                for d in range(D):
+                    nc.tensor.matmul(
+                        bank[:, t, :], lhsT=cone4[t][:, d, h, :], rhs=ident[:], is_transpose=True,
+                        start=(d == 0), stop=(d == D - 1),
+                    )
+            nc.scalar.activation(out=knee_t[:, h], in_=bank[:], func=ACT.Copy, scale=-KNEE)
+        knee = keep.tile([P, HALVES, PACK, P], F32, name="knee")
+        for h in range(HALVES):
+            bank = psum.tile([P, PACK, P], F32, name="knee_back%d" % h, tag="bank%d" % (HALVES + h))
+            for t in range(PACK):
+                nc.tensor.transpose(bank[:, t, :], knee_t[:, h, t, :], ident[:])
+            nc.scalar.copy(out=knee[:, h], in_=bank[:])
+        inv = keep.tile([P, PACK, V], F32, name="inv")
+        nc.scalar.activation(out=inv[:], in_=log_sq[:], func=ACT.Sigmoid, scale=-1.0)
+
+        w2 = keep.tile([P, 2 * N], U8, name="w2", tag="slot_c", align_bytes=64)
+        nc.sync.dma_start(out=w2[:].bitcast(I32), in_=w2_words[0].bitcast(I32))
+        unit_sb = keep.tile([P, PACK], F32, name="unit_sb", tag="slot_e")
+        nc.sync.dma_start(out=unit_sb[:], in_=unit.rearrange("(p t) o -> p (t o)", t=PACK))
+        w2s = keep.tile([P, N], U8, name="w2s", tag="slot_d", align_bytes=64)
+        nc.vector.memset(w2s[:].bitcast(I32), 0)
+        for q in range(QUADS):
+            nc.sync.dma_start(
+                out=w2s[32 * q : 32 * q + ROWS, :].bitcast(I32),
+                in_=w2_scales[0, ROWS * q : ROWS * (q + 1), :].bitcast(I32),
+            )
 
         y = {}
         for h in range(HALVES):
@@ -90,7 +139,6 @@ def tile_picked_yphotn_log_p_kernel(
                 y[t, h] = psum.tile([P, BANK], F32, name="y%d%d" % (t, h), tag="bank%d" % (PACK * h + t))
         for o in range(PASSES):
             for h in range(HALVES):
-                cols = slice(h * BANK, (h + 1) * BANK)
                 xg = keep.tile([P, BANK], U32, name="xg%d%d" % (o, h), align_bytes=64)
                 nc.vector.tensor_copy(
                     out=xg[:], in_=x_win[o][:].indirect(offs_sb[:, h * BANK // 16 : (h + 1) * BANK // 16])
@@ -101,85 +149,80 @@ def tile_picked_yphotn_log_p_kernel(
                         lhsT=w1d[:, o, t].rearrange("p m b -> p (m b)").bitcast(FP4X4),
                         lhsT_scale=w1sd[:, o, t, :],
                         rhs=xg[:].bitcast(FP8X4),
-                        rhs_scale=xs[o][:, cols],
+                        rhs_scale=xs[:, o * S + h * BANK : o * S + (h + 1) * BANK],
                         start=(o == 0),
                         stop=(o == PASSES - 1),
                     )
-
-        late = keep.tile([P, 3 * S + PACK * U], F32, name="late", tag="slot_c", align_bytes=64)
-        for t in range(1, PACK):
-            nc.sync.dma_start(out=late[:, (t - 1) * S : t * S], in_=dist_rows[:, t, :])
-        nc.sync.dma_start(out=late[:, 3 * S :], in_=brdf.rearrange("(p t) r -> p (t r)", t=PACK))
-        dist_sb = [dist_a[:]] + [late[:, (t - 1) * S : t * S] for t in range(1, PACK)]
-
-        unit_sb = keep.tile([P, PACK], F32, name="unit_sb")
-        nc.gpsimd.dma_start(out=unit_sb[:], in_=unit.rearrange("(p t) o -> p (t o)", t=PACK))
-        w2 = keep.tile([P, 2 * N], U8, name="w2", align_bytes=64)
-        nc.gpsimd.dma_start(out=w2[:].bitcast(I32), in_=w2_words[0].bitcast(I32))
-        for q in range(QUADS):
-            nc.gpsimd.dma_start(
-                out=w2s[32 * q : 32 * q + ROWS, :].bitcast(I32),
-                in_=w2_scales[0, ROWS * q : ROWS * (q + 1), :].bitcast(I32),
-            )
+        brdf_sb = keep.tile([P, PACK * U], F32, name="brdf_sb", tag="slot_a", align_bytes=64)
+        nc.sync.dma_start(out=brdf_sb[:], in_=brdf.rearrange("(p t) r -> p (t r)", t=PACK))
 
         sig = [keep.tile([P, D, HALVES, BANK // D], F32, name="sig%d" % t) for t in range(PACK)]
+        num_t = {}
         for h in range(HALVES):
             for t in range(PACK):
-                nc.scalar.activation(
-                    out=sig[t][:, :, h, :], in_=y[t, h][:].rearrange("p (v d) -> p d v", d=D), func=ACT.Sigmoid, scale=-1.0
+                y_dv = y[t, h][:].rearrange("p (v d) -> p d v", d=D)
+                nc.scalar.activation(out=sig[t][:, :, h, :], in_=y_dv, func=ACT.Sigmoid, scale=-1.0)
+                if h == HALVES - 1:
+                    nc.vector.tensor_scalar(out=sig[t][:], in0=sig[t][:], scalar1=SIG_FLOOR, scalar2=None, op0=ALU.max)
+                above = keep.tile([P, D, P], F32, name="above%d%d" % (t, h))
+                nc.vector.scalar_tensor_tensor(
+                    out=above[:], in0=y_dv, scalar=KNEE, in1=cone4[t][:, :, h, :], op0=ALU.max, op1=ALU.mult
                 )
-
-        rad = keep.tile([P, PACK, V], F32, name="rad")
-        slope = [keep.tile([P, S], F32, name="slope%d" % t) for t in range(PACK)]
-        for t in range(PACK):
-            nc.vector.tensor_reduce(
-                out=rad[:, t, :], in_=dist_sb[t].rearrange("p (v d) -> p v d", d=D), axis=mybir.AxisListType.X, op=ALU.max
-            )
-            nc.gpsimd.tensor_scalar(
-                out=slope[t][:].rearrange("p (d c i) -> p c d i", d=D, i=4),
-                in0=dist_sb[t].rearrange("p (c i d) -> p c d i", d=D, i=4),
-                scalar1=-1.0, scalar2=1.0, op0=ALU.mult, op1=ALU.add,
-            )
-        rad_sq = keep.tile([P, PACK, V], F32, name="rad_sq")
-        nc.vector.tensor_tensor(out=rad_sq[:], in0=rad[:], in1=rad[:], op=ALU.mult)
+                num_t[t, h] = psum.tile([P, P], F32, name="num_t%d%d" % (t, h), tag="bank%d" % (PACK * h + t))
+                for d in range(D):
+                    nc.tensor.matmul(
+                        num_t[t, h][:], lhsT=above[:, d, :], rhs=ident[:], is_transpose=True, start=(d == 0), stop=False
+                    )
+                nc.tensor.matmul(
+                    num_t[t, h][:], lhsT=knee[:, h, t, :], rhs=ident[:], is_transpose=True, start=False, stop=False
+                )
 
         logsig = [keep.tile([P, D, HALVES, BANK // D], F32, name="logsig%d" % t) for t in range(PACK)]
         for t in range(PACK):
-            nc.scalar.activation(out=logsig[t][:], in_=sig[t][:], func=ACT.Ln, bias=TINY)
-        log_sq = keep.tile([P, PACK, V], F32, name="log_sq")
-        nc.scalar.activation(out=log_sq[:], in_=rad_sq[:], func=ACT.Ln, scale=5.0, bias=TINY)
-        inv = keep.tile([P, PACK, V], F32, name="inv")
-        nc.scalar.activation(out=inv[:], in_=log_sq[:], func=ACT.Sigmoid, scale=-1.0)
+            for h in range(HALVES):
+                nc.scalar.activation(out=logsig[t][:, :, h, :], in_=sig[t][:, :, h, :], func=ACT.Ln)
+
+        est = []
+        for t in range(PACK):
+            window = keep.tile([P, 2 * V], F32, name="est%d" % t)
+            for h in range(HALVES):
+                below = keep.tile([P, D, P], F32, name="below%d%d" % (t, h))
+                nc.vector.scalar_tensor_tensor(
+                    out=below[:], in0=logsig[t][:, :, h, :], scalar=-1.0, in1=cone4[t][:, :, h, :],
+                    op0=ALU.mult, op1=ALU.mult,
+                )
+                for d in range(D):
+                    nc.tensor.matmul(
+                        num_t[t, h][:], lhsT=below[:, d, :], rhs=ident[:], is_transpose=True, start=False, stop=(d == D - 1)
+                    )
+            for h in range(HALVES):
+                nc.vector.tensor_copy(out=window[:, V + h * P : V + (h + 1) * P], in_=num_t[t, h][:])
+            num = psum.tile([P, V], F32, name="num%d" % t, tag="bank%d" % t)
+            for h in range(HALVES):
+                nc.tensor.transpose(num[:, h * P : (h + 1) * P], window[:, V + h * P : V + (h + 1) * P], ident[:])
+            nc.vector.tensor_tensor(out=window[:, :V], in0=num[:], in1=inv[:, t, :], op=ALU.mult)
+            est.append(window)
 
         hid = keep.tile([P, PACK, U], BF16, name="hid", align_bytes=64)
         for t in range(PACK):
-            nflux = keep.tile([P, D, HALVES, BANK // D], F32, name="nflux%d" % t)
-            for h in range(HALVES):
-                nc.vector.scalar_tensor_tensor(
-                    out=nflux[:, :, h, :], in0=y[t, h][:].rearrange("p (v d) -> p d v", d=D), scalar=-1.0,
-                    in1=logsig[t][:, :, h, :], op0=ALU.mult, op1=ALU.min,
-                )
-            fw = keep.tile([P, S], F32, name="fw%d" % t)
-            nc.vector.scalar_tensor_tensor(
-                out=fw[:], in0=slope[t][:], scalar=0.0, in1=nflux[:].rearrange("p d h v -> p (d h v)"),
-                op0=ALU.max, op1=ALU.mult,
-            )
-            est = keep.tile([P, 3 * V], F32, name="est%d" % t)
-            nc.vector.tensor_tensor(out=est[:, V:], in0=fw[:, : 2 * V], in1=fw[:, 2 * V :], op=ALU.add)
-            num = keep.tile([P, V], F32, name="num%d" % t)
-            nc.vector.tensor_tensor(out=num[:], in0=est[:, V : 2 * V], in1=est[:, 2 * V :], op=ALU.add)
-            nc.vector.tensor_tensor(out=est[:, :V], in0=num[:], in1=inv[:, t, :], op=ALU.mult)
             ep = keep.tile([P, U], F32, name="ep%d" % t)
-            nc.scalar.activation(out=ep[:], in_=est[:].indirect(pix_sb[:]), func=ACT.Copy)
             rad2 = keep.tile([P, U], F32, name="rad2%d" % t)
-            nc.vector.tensor_tensor(
-                out=rad2[:], in0=ep[:], in1=late[:, 3 * S + t * U : 3 * S + (t + 1) * U], op=ALU.mult
-            )
             logr = keep.tile([P, U], F32, name="logr%d" % t)
-            nc.scalar.activation(out=logr[:], in_=rad2[:], func=ACT.Ln, scale=-5.0, bias=0.3)
-            nc.vector.tensor_scalar(
-                out=hid[:, t, :], in0=logr[:], scalar1=unit_sb[:, t : t + 1], scalar2=None, op0=ALU.mult
-            )
+            for c0 in range(0, U, PIX_HALF):
+                nc.scalar.activation(
+                    out=ep[:, c0 : c0 + PIX_HALF],
+                    in_=est[t][:].indirect(pix_sb[:, c0 // 16 : (c0 + PIX_HALF) // 16]), func=ACT.Copy,
+                )
+            width = PIX_HALF if t == PACK - 1 else U
+            for c0 in range(0, U, width):
+                cols = slice(c0, c0 + width)
+                nc.vector.tensor_tensor(
+                    out=rad2[:, cols], in0=ep[:, cols], in1=brdf_sb[:, t * U + c0 : t * U + c0 + width], op=ALU.mult
+                )
+                nc.scalar.activation(out=logr[:, cols], in_=rad2[:, cols], func=ACT.Ln, scale=5.0, bias=0.3)
+                nc.vector.tensor_scalar(
+                    out=hid[:, t, cols], in0=logr[:, cols], scalar1=unit_sb[:, t : t + 1], scalar2=None, op0=ALU.mult
+                )
 
         out_rows = out.rearrange("(b p) r -> p b r", p=P)
         for g in range(U // PIX_HALF):
@@ -196,7 +239,7 @@ def tile_picked_yphotn_log_p_kernel(
             )
             res = keep.tile([P, N // P, PIX_HALF], F32, name="res%d" % g)
             for b in range(N // P):
-                acc = psum.tile([P, PIX_HALF], F32, name="acc%d%d" % (g, b), tag="bank%d" % (2 * g + b))
+                acc = psum.tile([P, PIX_HALF], F32, name="acc%d%d" % (g, b), tag="bank%d" % (PACK + 2 * g + b))
                 nc.tensor.matmul_mx(
                     out=acc[:],
                     lhsT=w2[:, 2 * P * b : 2 * P * (b + 1)].bitcast(FP4X4),
@@ -206,8 +249,8 @@ def tile_picked_yphotn_log_p_kernel(
                     start=True,
                     stop=True,
                 )
-                if b == 0:
+                if b == 0 or g == 0:
                     nc.scalar.copy(out=res[:, b, :], in_=acc[:])
                 else:
                     nc.vector.tensor_copy(out=res[:, b, :], in_=acc[:])
-            nc.sync.dma_start(out=out_rows[:, :, cols], in_=res[:])
+                nc.sync.dma_start(out=out_rows[:, b, cols], in_=res[:, b, :])

import math
from contextlib import ExitStack

import concourse.mybir as mybir
from concourse.masks import make_identity

K, T, S, D, N, H, V, U = 1024, 4096, 1024, 4, 256, 512, 256, 512
FLOPS = 2 * K * H * S + 2 * H * N * U

F32 = mybir.dt.float32
BF16 = mybir.dt.bfloat16
I32 = mybir.dt.int32
U32 = mybir.dt.uint32
U16 = mybir.dt.uint16
U8 = mybir.dt.uint8
FP8X4 = mybir.dt.float8_e4m3fn_x4
FP4X4 = mybir.dt.float4_e2m1fn_x4
ALU = mybir.AluOpType
ACT = mybir.ActivationFunctionType

P = 128
PACK = 4
PASSES = K // (P * PACK)
BANK = 512
HALVES = S // BANK
QUADS = 4
ROWS = 4
TINY = 2.0 ** -60
PIX_HALF = U // 2
KNEE = 16.0
SIG_FLOOR = 1.0 / (1.0 + math.exp(KNEE))


def tile_picked_yphotn_log_p_kernel(
    tc, x_words, x_scales, w1_words, w1_scales, dist, brdf, unit, w2_words, w2_scales, offs, pix, out
):
    nc = tc.nc
    dist_rows = dist.rearrange("(p t) j -> p t j", t=PACK)

    with ExitStack() as ctx:
        keep = ctx.enter_context(tc.tile_pool(name="keep", bufs=1))
        psum = ctx.enter_context(tc.psum_pool(name="psum", bufs=1))

        ident = keep.tile([P, P], F32, name="ident")
        make_identity(nc, ident[:])

        offs_sb = keep.tile([P, S // 16], U16, name="offs_sb")
        nc.sync.dma_start(offs_sb[:], offs)
        w1_raw = keep.tile([P, PASSES, 2 * H], U8, name="w1_raw", tag="slot_a", align_bytes=64)
        nc.sync.dma_start(out=w1_raw[:].bitcast(I32), in_=w1_words.rearrange("o p b -> p o b").bitcast(I32))
        pix_sb = keep.tile([P, U // 16], U16, name="pix_sb")
        nc.sync.dma_start(pix_sb[:], pix)
        dist_sb = [keep.tile([P, S], F32, name="dist%d" % t, tag="dist%d" % t) for t in range(PACK)]
        nc.sync.dma_start(out=dist_sb[0][:], in_=dist_rows[:, 0, :])

        xs_win = keep.tile([P, T], U8, name="xs_win", tag="slot_b", align_bytes=64)
        nc.vector.memset(xs_win[:].bitcast(I32), 0)
        nc.sync.dma_start(out=xs_win[0:P:4, :].bitcast(I32), in_=x_scales.rearrange("o s n -> s o n").bitcast(I32))
        for t in range(1, PACK):
            nc.sync.dma_start(out=dist_sb[t][:], in_=dist_rows[:, t, :])
        w1s_raw = keep.tile([P, PASSES * H], U8, name="w1s_raw", tag="slot_c", align_bytes=64)
        nc.vector.memset(w1s_raw[:].bitcast(I32), 0)
        for q in range(QUADS):
            nc.sync.dma_start(
                out=w1s_raw[32 * q : 32 * q + ROWS, :].bitcast(I32),
                in_=w1_scales[:, ROWS * q : ROWS * (q + 1), :].rearrange("o r n -> r o n").bitcast(I32),
            )
        xs = keep.tile([P, PASSES * S], U8, name="xs", align_bytes=64)
        nc.vector.memset(xs[:].bitcast(I32), 0)

        w1d = keep.tile([P, PASSES, PACK, P, 2], U8, name="w1d", align_bytes=64)
        nc.vector.tensor_copy(out=w1d[:], in_=w1_raw[:].rearrange("p o (m t b) -> p o t m b", t=PACK, b=2))
        x_first = keep.tile([P, T], U32, name="x_first", tag="slot_a", align_bytes=64)
        nc.sync.dma_start(out=x_first[:].bitcast(I32), in_=x_words[0].rearrange("p n t -> p (n t)").bitcast(I32))
        xs_spread = keep.tile([P, S], U8, name="xs_spread", tag="slot_d", align_bytes=64)
        nc.vector.tensor_copy(out=xs_spread[:], in_=xs_win[:].indirect(offs_sb[:]))
        for q in range(QUADS):
            nc.sync.dma_start(
                out=xs[32 * q : 32 * q + ROWS, :].bitcast(I32),
                in_=xs_spread[32 * q : 32 * (q + 1) : 4, :].bitcast(I32),
            )
        x_second = keep.tile([P, T], U32, name="x_second", tag="slot_b", align_bytes=64)
        nc.sync.dma_start(out=x_second[:].bitcast(I32), in_=x_words[1].rearrange("p n t -> p (n t)").bitcast(I32))
        x_win = [x_first, x_second]
        w1sd = keep.tile([P, PASSES, PACK, P], U8, name="w1sd", align_bytes=64)
        nc.vector.tensor_copy(out=w1sd[:], in_=w1s_raw[:].rearrange("p (o m t) -> p o t m", o=PASSES, t=PACK))

        rad = keep.tile([P, PACK, V], F32, name="rad")
        cone = [keep.tile([P, S], F32, name="cone%d" % t) for t in range(PACK)]
        for t in range(PACK):
            nc.vector.tensor_reduce(
                out=rad[:, t, :], in_=dist_sb[t][:].rearrange("p (v d) -> p v d", d=D), axis=mybir.AxisListType.X, op=ALU.max
            )
            nc.scalar.activation(
                out=cone[t][:].rearrange("p (d c i) -> p c d i", d=D, i=4),
                in_=dist_sb[t][:].rearrange("p (c i d) -> p c d i", d=D, i=4),
                func=ACT.Relu, scale=-1.0, bias=1.0,
            )
        rad_sq = keep.tile([P, PACK, V], F32, name="rad_sq", tag="slot_e")
        log_sq = keep.tile([P, PACK, V], F32, name="log_sq")
        for t in range(PACK):
            nc.scalar.activation(out=rad_sq[:, t, :], in_=rad[:, t, :], func=ACT.Square)
            nc.scalar.activation(out=log_sq[:, t, :], in_=rad_sq[:, t, :], func=ACT.Ln, scale=5.0, bias=TINY)
        cone4 = [c[:].rearrange("p (d h v) -> p d h v", d=D, h=HALVES) for c in cone]
        knee_t = keep.tile([P, HALVES, PACK, P], F32, name="knee_t")
        for h in range(HALVES):
            bank = psum.tile([P, PACK, P], F32, name="cone_sum%d" % h, tag="bank%d" % h)
            for t in range(PACK):
                for d in range(D):
                    nc.tensor.matmul(
                        bank[:, t, :], lhsT=cone4[t][:, d, h, :], rhs=ident[:], is_transpose=True,
                        start=(d == 0), stop=(d == D - 1),
                    )
            nc.scalar.activation(out=knee_t[:, h], in_=bank[:], func=ACT.Copy, scale=-KNEE)
        knee = keep.tile([P, HALVES, PACK, P], F32, name="knee")
        for h in range(HALVES):
            bank = psum.tile([P, PACK, P], F32, name="knee_back%d" % h, tag="bank%d" % (HALVES + h))
            for t in range(PACK):
                nc.tensor.transpose(bank[:, t, :], knee_t[:, h, t, :], ident[:])
            nc.scalar.copy(out=knee[:, h], in_=bank[:])
        inv = keep.tile([P, PACK, V], F32, name="inv")
        nc.scalar.activation(out=inv[:], in_=log_sq[:], func=ACT.Sigmoid, scale=-1.0)

        w2 = keep.tile([P, 2 * N], U8, name="w2", tag="slot_c", align_bytes=64)
        nc.sync.dma_start(out=w2[:].bitcast(I32), in_=w2_words[0].bitcast(I32))
        unit_sb = keep.tile([P, PACK], F32, name="unit_sb", tag="slot_e")
        nc.sync.dma_start(out=unit_sb[:], in_=unit.rearrange("(p t) o -> p (t o)", t=PACK))
        w2s = keep.tile([P, N], U8, name="w2s", tag="slot_d", align_bytes=64)
        nc.vector.memset(w2s[:].bitcast(I32), 0)
        for q in range(QUADS):
            nc.sync.dma_start(
                out=w2s[32 * q : 32 * q + ROWS, :].bitcast(I32),
                in_=w2_scales[0, ROWS * q : ROWS * (q + 1), :].bitcast(I32),
            )

        y = {}
        for h in range(HALVES):
            for t in range(PACK):
                y[t, h] = psum.tile([P, BANK], F32, name="y%d%d" % (t, h), tag="bank%d" % (PACK * h + t))
        for o in range(PASSES):
            for h in range(HALVES):
                xg = keep.tile([P, BANK], U32, name="xg%d%d" % (o, h), align_bytes=64)
                nc.vector.tensor_copy(
                    out=xg[:], in_=x_win[o][:].indirect(offs_sb[:, h * BANK // 16 : (h + 1) * BANK // 16])
                )
                for t in range(PACK):
                    nc.tensor.matmul_mx(
                        out=y[t, h][:],
                        lhsT=w1d[:, o, t].rearrange("p m b -> p (m b)").bitcast(FP4X4),
                        lhsT_scale=w1sd[:, o, t, :],
                        rhs=xg[:].bitcast(FP8X4),
                        rhs_scale=xs[:, o * S + h * BANK : o * S + (h + 1) * BANK],
                        start=(o == 0),
                        stop=(o == PASSES - 1),
                    )
        brdf_sb = keep.tile([P, PACK * U], F32, name="brdf_sb", tag="slot_a", align_bytes=64)
        nc.sync.dma_start(out=brdf_sb[:], in_=brdf.rearrange("(p t) r -> p (t r)", t=PACK))

        sig = [keep.tile([P, D, HALVES, BANK // D], F32, name="sig%d" % t) for t in range(PACK)]
        num_t = {}
        for h in range(HALVES):
            for t in range(PACK):
                y_dv = y[t, h][:].rearrange("p (v d) -> p d v", d=D)
                nc.scalar.activation(out=sig[t][:, :, h, :], in_=y_dv, func=ACT.Sigmoid, scale=-1.0)
                if h == HALVES - 1:
                    nc.vector.tensor_scalar(out=sig[t][:], in0=sig[t][:], scalar1=SIG_FLOOR, scalar2=None, op0=ALU.max)
                above = keep.tile([P, D, P], F32, name="above%d%d" % (t, h))
                nc.vector.scalar_tensor_tensor(
                    out=above[:], in0=y_dv, scalar=KNEE, in1=cone4[t][:, :, h, :], op0=ALU.max, op1=ALU.mult
                )
                num_t[t, h] = psum.tile([P, P], F32, name="num_t%d%d" % (t, h), tag="bank%d" % (PACK * h + t))
                for d in range(D):
                    nc.tensor.matmul(
                        num_t[t, h][:], lhsT=above[:, d, :], rhs=ident[:], is_transpose=True, start=(d == 0), stop=False
                    )
                nc.tensor.matmul(
                    num_t[t, h][:], lhsT=knee[:, h, t, :], rhs=ident[:], is_transpose=True, start=False, stop=False
                )

        logsig = [keep.tile([P, D, HALVES, BANK // D], F32, name="logsig%d" % t) for t in range(PACK)]
        for t in range(PACK):
            for h in range(HALVES):
                nc.scalar.activation(out=logsig[t][:, :, h, :], in_=sig[t][:, :, h, :], func=ACT.Ln)

        est = []
        for t in range(PACK):
            window = keep.tile([P, 2 * V], F32, name="est%d" % t)
            for h in range(HALVES):
                below = keep.tile([P, D, P], F32, name="below%d%d" % (t, h))
                nc.vector.scalar_tensor_tensor(
                    out=below[:], in0=logsig[t][:, :, h, :], scalar=-1.0, in1=cone4[t][:, :, h, :],
                    op0=ALU.mult, op1=ALU.mult,
                )
                for d in range(D):
                    nc.tensor.matmul(
                        num_t[t, h][:], lhsT=below[:, d, :], rhs=ident[:], is_transpose=True, start=False, stop=(d == D - 1)
                    )
            for h in range(HALVES):
                nc.vector.tensor_copy(out=window[:, V + h * P : V + (h + 1) * P], in_=num_t[t, h][:])
            num = psum.tile([P, V], F32, name="num%d" % t, tag="bank%d" % t)
            for h in range(HALVES):
                nc.tensor.transpose(num[:, h * P : (h + 1) * P], window[:, V + h * P : V + (h + 1) * P], ident[:])
            nc.vector.tensor_tensor(out=window[:, :V], in0=num[:], in1=inv[:, t, :], op=ALU.mult)
            est.append(window)

        hid = keep.tile([P, PACK, U], BF16, name="hid", align_bytes=64)
        for t in range(PACK):
            ep = keep.tile([P, U], F32, name="ep%d" % t)
            rad2 = keep.tile([P, U], F32, name="rad2%d" % t)
            logr = keep.tile([P, U], F32, name="logr%d" % t)
            for c0 in range(0, U, PIX_HALF):
                nc.scalar.activation(
                    out=ep[:, c0 : c0 + PIX_HALF],
                    in_=est[t][:].indirect(pix_sb[:, c0 // 16 : (c0 + PIX_HALF) // 16]), func=ACT.Copy,
                )
            width = PIX_HALF if t == PACK - 1 else U
            for c0 in range(0, U, width):
                cols = slice(c0, c0 + width)
                nc.vector.tensor_tensor(
                    out=rad2[:, cols], in0=ep[:, cols], in1=brdf_sb[:, t * U + c0 : t * U + c0 + width], op=ALU.mult
                )
                nc.scalar.activation(out=logr[:, cols], in_=rad2[:, cols], func=ACT.Ln, scale=5.0, bias=0.3)
                nc.vector.tensor_scalar(
                    out=hid[:, t, cols], in0=logr[:, cols], scalar1=unit_sb[:, t : t + 1], scalar2=None, op0=ALU.mult
                )

        out_rows = out.rearrange("(b p) r -> p b r", p=P)
        for g in range(U // PIX_HALF):
            cols = slice(g * PIX_HALF, (g + 1) * PIX_HALF)
            woven = keep.tile([P, PIX_HALF, PACK], BF16, name="woven%d" % g, align_bytes=64)
            nc.vector.tensor_copy(
                out=woven[:].rearrange("p (c i) t -> p c t i", i=4),
                in_=hid[:, :, cols].rearrange("p t (c i) -> p c t i", i=4),
            )
            codes = keep.tile([P, PIX_HALF], U32, name="codes%d" % g, align_bytes=64)
            scales = keep.tile([P, PIX_HALF], U8, name="scales%d" % g, align_bytes=64)
            nc.vector.quantize_mx(
                out=codes[:].bitcast(FP8X4), scales=scales[:], in_=woven[:].rearrange("p r t -> p (r t)")
            )
            res = keep.tile([P, N // P, PIX_HALF], F32, name="res%d" % g)
            for b in range(N // P):
                acc = psum.tile([P, PIX_HALF], F32, name="acc%d%d" % (g, b), tag="bank%d" % (PACK + 2 * g + b))
                nc.tensor.matmul_mx(
                    out=acc[:],
                    lhsT=w2[:, 2 * P * b : 2 * P * (b + 1)].bitcast(FP4X4),
                    lhsT_scale=w2s[:, P * b : P * (b + 1)],
                    rhs=codes[:].bitcast(FP8X4),
                    rhs_scale=scales[:],
                    start=True,
                    stop=True,
                )
                if b == 0 or g == 0:
                    nc.scalar.copy(out=res[:, b, :], in_=acc[:])
                else:
                    nc.vector.tensor_copy(out=res[:, b, :], in_=acc[:])
                nc.sync.dma_start(out=out_rows[:, b, cols], in_=res[:, b, :])
